import numpy as np
import ml_dtypes


def mxq(x, axis, fmt="e4m3"):
    dtype, down = {"e4m3": (ml_dtypes.float8_e4m3fn, 7), "e5m2": (ml_dtypes.float8_e5m2, 14)}[fmt]
    v = np.moveaxis(np.asarray(x, np.float32).astype(ml_dtypes.bfloat16).astype(np.float64), axis, -1)
    blocks = v.reshape(v.shape[:-1] + (-1, 32))
    amax = np.abs(blocks).max(-1, keepdims=True)
    byte = np.maximum(np.where(amax > 0, np.frexp(amax)[1] - 1 + 127, 0) - down, 1)
    scale = np.exp2(byte - 127.0)
    codes = (blocks / scale).astype(np.float32).astype(dtype).astype(np.float64)
    return np.moveaxis((codes * scale).reshape(v.shape), -1, axis)


WIDE = False


def mx_kscale(k):
    if not WIDE:
        return np.ones(k)
    levels = np.array([10, -10, 5, -5, 0])
    if k % 512:
        return np.exp2(np.random.permutation(np.resize(levels, k // 32))).repeat(32)
    a = np.empty((k // 512, 16))
    for p in range(k // 512):
        a[p, :8] = np.random.permutation(np.resize(levels, 8))
        for g in range(8):
            far = levels[np.abs(levels - a[p, g]) >= 10]
            a[p, g + 8] = far[np.random.randint(len(far))]
    return np.exp2(a.ravel()).repeat(32)


def f64(x):
    return np.asarray(x).astype(np.float64)


def striped(idx):
    return np.tile(idx.reshape(-1, 16).T, (8, 1)).astype(np.uint16)


def unstriped(offs):
    return offs[:16].T.reshape(-1).astype(np.int64)


def striped8(idx):
    return np.concatenate([x.reshape(-1, 16).T for x in idx]).astype(np.uint16)


def runs(offs, k):
    lists = np.stack([offs[16 * r : 16 * r + 16].T.reshape(-1) for r in range(8)]).astype(np.int64)
    return lists[np.arange(k) % 512 // 64]


def pack_weight(w):
    k, n = w.shape
    w = f64(np.asarray(w, np.float32).astype(ml_dtypes.bfloat16)).reshape(k // 32, 32, n)
    amax = np.abs(w).max(1)
    byte = np.clip(np.where(amax > 0, np.frexp(amax)[1] - 1 + 127 - 7, 1), 1, 254)
    scaled = (w * np.exp2(127.0 - byte)[:, None, :]).reshape(k, n).astype(np.float32)
    words = np.ascontiguousarray(scaled.reshape(k // 512, 128, 4, n).transpose(0, 1, 3, 2)).astype(ml_dtypes.float8_e4m3fn).view(np.uint8)
    return words, np.ascontiguousarray(byte.astype(np.uint8).reshape(k // 512, 16, n))


def unpack_weight(words, scales):
    g, p, n, _ = words.shape
    vals = np.ascontiguousarray(words).view(ml_dtypes.float8_e4m3fn).astype(np.float64) * np.repeat(np.exp2(scales.astype(np.float64) - 127.0), 8, axis=1)[..., None]
    return vals.transpose(0, 1, 3, 2).reshape(g * 512, n)


K, T, S, H, C = 512, 2048, 512, 512, 512
P = 2 ** 7


def setup_inputs():
    n = np.random.standard_normal
    s = mx_kscale(K)[:, None]
    packed_xT = pack_weight(n((K, T)) * s)
    return {
        "x_words": packed_xT[0],
        "x_scales": packed_xT[1],
        "w1": (n((K, H)) / np.sqrt(K) / s).astype(np.float32),
        "w2": (n((K, H)) / np.sqrt(K) / s).astype(np.float32),
        "tr1": np.tile(np.random.uniform(-1, 1, S), (P, 1)).astype(np.float32),
        "tr2": np.tile(np.random.uniform(-1, 1, S), (P, 1)).astype(np.float32),
        "tr3": np.tile(np.random.uniform(-1, 1, S), (P, 1)).astype(np.float32),
        "gs": (np.random.uniform(0.5, 1.5, (K, 1)) / s).astype(np.float32),
        "offs": striped(np.random.permutation(T)[:S]),
        "two": striped(np.random.permutation(T)[:S]),
        "s1": striped8(np.stack([np.random.permutation(S) for _ in range(8)])),
        "s2": striped8(np.stack([np.random.permutation(S) for _ in range(8)])),
        "s3": striped8(np.stack([np.random.permutation(S) for _ in range(8)])),
        "cand": striped(np.random.permutation(T)[:C]),
    }


def reference(x_words, x_scales, w1, w2, tr1, tr2, tr3, gs, offs, two, s1, s2, s3, cand):
    x_cand = unpack_weight(x_words, x_scales)[:, unstriped(cand)]
    x_two = unpack_weight(x_words, x_scales)[:, unstriped(two)]
    c = mxq(f64(w2), 0, "e4m3").T @ x_two
    xq = unpack_weight(x_words, x_scales)[:, unstriped(offs)]
    y = mxq(f64(w1), 0, "e4m3").T @ xq
    z = f64(gs) * (c + np.maximum(np.maximum(y[np.arange(H)[:, None], runs(s1, H)] + f64(tr1)[:1], y[np.arange(H)[:, None], runs(s2, H)] + f64(tr2)[:1]), y[np.arange(H)[:, None], runs(s3, H)] + f64(tr3)[:1]))
    return 0.0625 * ((x_cand.T @ mxq(z, 0, "e4m3")))

@@ -1,0 +1,211 @@
+from contextlib import ExitStack
+
+import concourse.mybir as mybir
+
+K, T, S, H, C = 512, 2048, 512, 512, 512
+FLOPS = 3 * 2 * 512 * 512 * 512
+
+F32 = mybir.dt.float32
+BF16 = mybir.dt.bfloat16
+I32 = mybir.dt.int32
+U32 = mybir.dt.uint32
+U16 = mybir.dt.uint16
+U8 = mybir.dt.uint8
+FP8X4 = mybir.dt.float8_e4m3fn_x4
+ADD = mybir.AluOpType.add
+MULT = mybir.AluOpType.mult
+MAX = mybir.AluOpType.max
+COPY = mybir.ActivationFunctionType.Copy
+
+P = 128
+PACK = 4
+CHUNKS = (256, 128, 128)
+
+
+def tile_picked_viterb3_none_p_kernel(
+    tc, x_words, x_scales, w1, w2, tr1, tr2, tr3, gs, offs, two, s1, s2, s3, cand, out
+):
+    nc = tc.nc
+    with ExitStack() as ctx:
+        keep = ctx.enter_context(tc.tile_pool(name="keep", bufs=1))
+        work = ctx.enter_context(tc.tile_pool(name="work", bufs=2))
+        psum = ctx.enter_context(tc.psum_pool(name="psum", bufs=4))
+
+        def load_list(src, name):
+            tile = keep.tile([P, S // 16], U16, name=name)
+            nc.sync.dma_start(tile[:], src)
+            return tile
+
+        table_scales = keep.tile([P, T], U8, name="table_scales", align_bytes=64)
+        nc.vector.memset(table_scales[:].bitcast(I32), 0)
+        offs_sb = load_list(offs, "offs_sb")
+        for q in range(4):
+            nc.sync.dma_start(
+                table_scales[32 * q : 32 * q + 4, :].bitcast(I32),
+                x_scales[0, 4 * q : 4 * q + 4, :].bitcast(I32),
+            )
+        table_words = keep.tile([P, T], U32, name="table_words", align_bytes=64)
+        nc.sync.dma_start(
+            table_words[:].bitcast(I32), x_words[0].rearrange("p n t -> p (n t)").bitcast(I32)
+        )
+        two_sb = load_list(two, "two_sb")
+        cand_sb = load_list(cand, "cand_sb")
+
+        HALVES = 2
+        HC = H // HALVES
+
+        def load_weight(w, name):
+            rows = w.rearrange("(p j) c -> p j c", j=PACK)
+            halves = []
+            for h in range(HALVES):
+                raw = keep.tile([P, PACK, HC], F32, name="%s_raw%d" % (name, h))
+                nc.sync.dma_start(raw[:], rows[:, :, h * HC : (h + 1) * HC])
+                halves.append(raw)
+            return halves
+
+        w1_raw = load_weight(w1, "w1")
+        s_sb = [load_list(s, "s%d_sb" % i) for i, s in enumerate((s1, s2, s3))]
+        tr_sb = []
+        for i, tr in enumerate((tr1, tr2, tr3)):
+            tile = keep.tile([P, S], F32, name="tr%d_sb" % i)
+            nc.sync.dma_start(tile[:], tr)
+            tr_sb.append(tile)
+        w2_raw = load_weight(w2, "w2")
+        gs_sb = keep.tile([P, PACK], F32, name="gs_sb")
+        nc.sync.dma_start(gs_sb[:], gs.rearrange("(p t) o -> p (t o)", t=PACK))
+
+        def pick(table, dtype, idx, name):
+            tile = keep.tile([P, S], dtype, name=name, align_bytes=64)
+            nc.vector.tensor_copy(tile[:], table[:].indirect(idx[:]))
+            return tile
+
+        def group_weight(halves, name):
+            grouped = keep.tile([P, PACK, P, PACK], BF16, name=name + "_grouped", align_bytes=64)
+            for h, raw in enumerate(halves):
+                m = slice(h * HC // PACK, (h + 1) * HC // PACK)
+                nc.scalar.copy(
+                    grouped[:, :, m, :].rearrange("p t m j -> p m j t"),
+                    raw[:].rearrange("p j (m t) -> p m j t", t=PACK),
+                )
+            return grouped
+
+        def quantize(grouped_flat, width, pool, name, tag):
+            codes = pool.tile([P, width], U32, name=name + "_codes", tag=tag + "_codes", align_bytes=64)
+            scales = pool.tile([P, width], U8, name=name + "_scales", tag=tag + "_scales", align_bytes=64)
+            nc.vector.quantize_mx(out=codes[:].bitcast(FP8X4), scales=scales[:], in_=grouped_flat)
+            return codes, scales
+
+        def product(acc, lhs, lhs_cols, rhs):
+            nc.tensor.matmul_mx(
+                out=acc,
+                lhsT=lhs[0][:, lhs_cols].bitcast(FP8X4),
+                lhsT_scale=lhs[1][:, lhs_cols],
+                rhs=rhs[0][:].bitcast(FP8X4),
+                rhs_scale=rhs[1][:],
+                start=True,
+                stop=True,
+            )
+
+        offs_scales = pick(table_scales, U8, offs_sb, "offs_scales")
+        two_scales = pick(table_scales, U8, two_sb, "two_scales")
+        cand_scales = pick(table_scales, U8, cand_sb, "cand_scales")
+        offs_words = pick(table_words, U32, offs_sb, "offs_words")
+        two_words = pick(table_words, U32, two_sb, "two_words")
+
+        w1_grouped = group_weight(w1_raw, "w1")
+        w1_q = quantize(w1_grouped[:].rearrange("p t m j -> p (t m j)"), H, keep, "w1", "w1")
+        cand_words = pick(table_words, U32, cand_sb, "cand_words")
+
+        y_sb = []
+        for t in range(PACK):
+            acc = psum.tile([P, S], F32, name="y_acc%d" % t, tag="acc")
+            product(acc[:], w1_q, slice(t * P, (t + 1) * P), (offs_words, offs_scales))
+            y = keep.tile([P, S], F32, name="y%d" % t)
+            nc.scalar.copy(y[:], acc[:])
+            y_sb.append(y)
+
+        w2_grouped = group_weight(w2_raw, "w2")
+        gc_sb = []
+
+        def emissions():
+            w2_q = quantize(w2_grouped[:].rearrange("p t m j -> p (t m j)"), H, keep, "w2", "w2")
+            for t in range(PACK):
+                acc = psum.tile([P, S], F32, name="c_acc%d" % t, tag="acc")
+                product(acc[:], w2_q, slice(t * P, (t + 1) * P), (two_words, two_scales))
+                gc = keep.tile([P, S], F32, name="gc%d" % t)
+                nc.scalar.activation(gc[:], acc[:], COPY, scale=gs_sb[:, t : t + 1])
+                gc_sb.append(gc)
+
+        starts = [sum(CHUNKS[:i]) for i in range(len(CHUNKS))]
+        state = {}
+
+        def gather(c, i, t):
+            n, j0 = CHUNKS[c], starts[c]
+            if t == 0:
+                state[c, i] = work.tile([P, PACK, n], F32, name="g%d_%d" % (c, i), tag="g%d" % i)
+            nc.vector.tensor_tensor(
+                state[c, i][:, t, :],
+                y_sb[t][:].indirect(s_sb[i][:, j0 // 16 : (j0 + n) // 16]),
+                tr_sb[i][:, j0 : j0 + n],
+                ADD,
+            )
+
+        def max12(c):
+            n = CHUNKS[c]
+            state[c, "m"] = work.tile([P, PACK, n], F32, name="m_%d" % c, tag="m")
+            nc.vector.tensor_tensor(state[c, "m"][:], state[c, 0][:], state[c, 1][:], MAX)
+
+        def max3(c):
+            n = CHUNKS[c]
+            state[c, "best"] = work.tile([P, PACK, n], F32, name="best_%d" % c, tag="best")
+            nc.vector.tensor_tensor(state[c, "best"][:], state[c, "m"][:], state[c, 2][:], MAX)
+
+        def weigh(c):
+            n, j0 = CHUNKS[c], starts[c]
+            z = work.tile([P, PACK, n], BF16, name="z_%d" % c, tag="z", align_bytes=64)
+            for t in range(PACK):
+                nc.vector.scalar_tensor_tensor(
+                    z[:, t, :], state[c, "best"][:, t, :], gs_sb[:, t : t + 1],
+                    gc_sb[t][:, j0 : j0 + n], MULT, ADD,
+                )
+            zg = work.tile([P, n, PACK], BF16, name="zg_%d" % c, tag="zg", align_bytes=64)
+            copy = nc.vector.tensor_copy if c == len(CHUNKS) - 1 else nc.scalar.copy
+            copy(
+                zg[:].rearrange("p (a i) t -> p a t i", i=4),
+                z[:].rearrange("p t (a i) -> p a t i", i=4),
+            )
+            state[c, "zg"] = zg
+
+        def score(c):
+            n, j0 = CHUNKS[c], starts[c]
+            z_q = quantize(state[c, "zg"][:].rearrange("p n t -> p (n t)"), n, work, "z%d" % c, "zq")
+            per_bank = 512 // n
+            res = work.tile([P, C // P, n], F32, name="res_%d" % c, tag="res")
+            for b0 in range(0, C // P, per_bank):
+                acc = psum.tile([P, per_bank, n], F32, name="o_acc%d_%d" % (c, b0), tag="oacc")
+                for b in range(per_bank):
+                    product(acc[:, b, :], (cand_words, cand_scales), slice((b0 + b) * P, (b0 + b + 1) * P), z_q)
+                nc.scalar.activation(res[:, b0 : b0 + per_bank, :], acc[:], COPY, scale=0.0625)
+            nc.sync.dma_start(out.rearrange("(b p) j -> p b j", p=P)[:, :, j0 : j0 + n], res[:])
+
+        last = len(CHUNKS) - 1
+        for c in range(len(CHUNKS)):
+            for t in range(PACK):
+                gather(c, 0, t)
+                if t == 0 and c > 0:
+                    max3(c - 1)
+                if t == 1 and c > 0:
+                    weigh(c - 1)
+            for t in range(PACK):
+                gather(c, 1, t)
+            if c == 0:
+                emissions()
+            gather(c, 2, 0)
+            max12(c)
+            if c > 0:
+                score(c - 1)
+            for t in range(1, PACK):
+                gather(c, 2, t)
+        max3(last)
+        weigh(last)
+        score(last)

@@ -1,6 +1,7 @@
 from contextlib import ExitStack
 
 import concourse.mybir as mybir
+from concourse.masks import make_identity
 
 K, T, S, H, C = 512, 2048, 512, 512, 512
 FLOPS = 3 * 2 * 512 * 512 * 512
@@ -15,11 +16,14 @@ FP8X4 = mybir.dt.float8_e4m3fn_x4
 ADD = mybir.AluOpType.add
 MULT = mybir.AluOpType.mult
 MAX = mybir.AluOpType.max
+SUB = mybir.AluOpType.subtract
+RELU = mybir.ActivationFunctionType.Relu
+IDENT = mybir.ActivationFunctionType.Identity
 COPY = mybir.ActivationFunctionType.Copy
 
 P = 128
 PACK = 4
-CHUNKS = (256, 128, 128)
+HALF = S // 2
 
 
 def tile_picked_viterb3_none_p_kernel(
@@ -29,7 +33,8 @@ def tile_picked_viterb3_none_p_kernel(
     with ExitStack() as ctx:
         keep = ctx.enter_context(tc.tile_pool(name="keep", bufs=1))
         work = ctx.enter_context(tc.tile_pool(name="work", bufs=2))
-        psum = ctx.enter_context(tc.psum_pool(name="psum", bufs=4))
+        psum = ctx.enter_context(tc.psum_pool(name="psum", bufs=2))
+        psum_fwd = ctx.enter_context(tc.psum_pool(name="psum_fwd", bufs=4))
 
         def load_list(src, name):
             tile = keep.tile([P, S // 16], U16, name=name)
@@ -44,12 +49,14 @@ def tile_picked_viterb3_none_p_kernel(
                 table_scales[32 * q : 32 * q + 4, :].bitcast(I32),
                 x_scales[0, 4 * q : 4 * q + 4, :].bitcast(I32),
             )
+        two_sb = load_list(two, "two_sb")
+        cand_sb = load_list(cand, "cand_sb")
         table_words = keep.tile([P, T], U32, name="table_words", align_bytes=64)
         nc.sync.dma_start(
             table_words[:].bitcast(I32), x_words[0].rearrange("p n t -> p (n t)").bitcast(I32)
         )
-        two_sb = load_list(two, "two_sb")
-        cand_sb = load_list(cand, "cand_sb")
+        ident = keep.tile([P, P], F32, name="ident")
+        make_identity(nc, ident[:])
 
         HALVES = 2
         HC = H // HALVES
@@ -58,29 +65,35 @@ def tile_picked_viterb3_none_p_kernel(
             rows = w.rearrange("(p j) c -> p j c", j=PACK)
             halves = []
             for h in range(HALVES):
-                raw = keep.tile([P, PACK, HC], F32, name="%s_raw%d" % (name, h))
+                raw = keep.tile([P, PACK, HC], F32, name="%s_raw%d" % (name, h), tag="%s_raw%d" % (name, h), align_bytes=64)
                 nc.sync.dma_start(raw[:], rows[:, :, h * HC : (h + 1) * HC])
                 halves.append(raw)
             return halves
 
         w1_raw = load_weight(w1, "w1")
         s_sb = [load_list(s, "s%d_sb" % i) for i, s in enumerate((s1, s2, s3))]
-        tr_sb = []
-        for i, tr in enumerate((tr1, tr2, tr3)):
-            tile = keep.tile([P, S], F32, name="tr%d_sb" % i)
-            nc.sync.dma_start(tile[:], tr)
-            tr_sb.append(tile)
         w2_raw = load_weight(w2, "w2")
         gs_sb = keep.tile([P, PACK], F32, name="gs_sb")
         nc.sync.dma_start(gs_sb[:], gs.rearrange("(p t) o -> p (t o)", t=PACK))
+        tr_col = []
+        for i, tr in enumerate((tr1, tr2, tr3)):
+            tile = keep.tile([P, S // P], F32, name="tr%d_col" % i)
+            with nc.allow_non_contiguous_dma(reason="one transition score a partition"):
+                nc.sync.dma_start(tile[:], tr[0].rearrange("(b p) -> p b", p=P))
+            tr_col.append(tile)
+        tr_over = [None]
+        for i in (1, 2):
+            tile = keep.tile([P, S // P], F32, name="tr%d_over" % i)
+            nc.gpsimd.tensor_tensor(tile[:], tr_col[i][:], tr_col[0][:], SUB)
+            tr_over.append(tile)
 
-        def pick(table, dtype, idx, name):
-            tile = keep.tile([P, S], dtype, name=name, align_bytes=64)
+        def pick(table, dtype, idx, name, tag=None):
+            tile = keep.tile([P, S], dtype, name=name, tag=tag or name, align_bytes=64)
             nc.vector.tensor_copy(tile[:], table[:].indirect(idx[:]))
             return tile
 
         def group_weight(halves, name):
-            grouped = keep.tile([P, PACK, P, PACK], BF16, name=name + "_grouped", align_bytes=64)
+            grouped = keep.tile([P, PACK, P, PACK], BF16, name=name + "_grouped", tag=name + "_grouped", align_bytes=64)
             for h, raw in enumerate(halves):
                 m = slice(h * HC // PACK, (h + 1) * HC // PACK)
                 nc.scalar.copy(
@@ -114,98 +127,142 @@ def tile_picked_viterb3_none_p_kernel(
 
         w1_grouped = group_weight(w1_raw, "w1")
         w1_q = quantize(w1_grouped[:].rearrange("p t m j -> p (t m j)"), H, keep, "w1", "w1")
-        cand_words = pick(table_words, U32, cand_sb, "cand_words")
+        cand_words = pick(table_words, U32, cand_sb, "cand_words", tag="w1_grouped")
 
         y_sb = []
         for t in range(PACK):
-            acc = psum.tile([P, S], F32, name="y_acc%d" % t, tag="acc")
+            acc = psum.tile([P, S], F32, name="y_acc%d" % t, tag="mx")
             product(acc[:], w1_q, slice(t * P, (t + 1) * P), (offs_words, offs_scales))
             y = keep.tile([P, S], F32, name="y%d" % t)
             nc.scalar.copy(y[:], acc[:])
             y_sb.append(y)
 
         w2_grouped = group_weight(w2_raw, "w2")
-        gc_sb = []
+        c_sb = []
 
         def emissions():
             w2_q = quantize(w2_grouped[:].rearrange("p t m j -> p (t m j)"), H, keep, "w2", "w2")
             for t in range(PACK):
-                acc = psum.tile([P, S], F32, name="c_acc%d" % t, tag="acc")
+                acc = psum.tile([P, S], F32, name="c_acc%d" % t, tag="mx")
                 product(acc[:], w2_q, slice(t * P, (t + 1) * P), (two_words, two_scales))
-                gc = keep.tile([P, S], F32, name="gc%d" % t)
-                nc.scalar.activation(gc[:], acc[:], COPY, scale=gs_sb[:, t : t + 1])
-                gc_sb.append(gc)
+                c_t = keep.tile([P, S], F32, name="c%d" % t)
+                nc.scalar.copy(c_t[:], acc[:])
+                c_sb.append(c_t)
 
-        starts = [sum(CHUNKS[:i]) for i in range(len(CHUNKS))]
-        state = {}
+        def turn(dst, sources):
+            for i, src in enumerate(sources):
+                nc.tensor.matmul(dst, src, ident[:], start=(i == 0), stop=(i == len(sources) - 1), is_transpose=True)
 
-        def gather(c, i, t):
-            n, j0 = CHUNKS[c], starts[c]
-            if t == 0:
-                state[c, i] = work.tile([P, PACK, n], F32, name="g%d_%d" % (c, i), tag="g%d" % i)
-            nc.vector.tensor_tensor(
-                state[c, i][:, t, :],
-                y_sb[t][:].indirect(s_sb[i][:, j0 // 16 : (j0 + n) // 16]),
-                tr_sb[i][:, j0 : j0 + n],
-                ADD,
+        def own(shape, dtype, name, tag=None):
+            return keep.tile(shape, dtype, name=name, tag=tag or name, align_bytes=64)
+
+        picked = {}
+
+        def gathers(i, half, tag=None, pieces=1):
+            g = own([P, PACK, HALF], F32, "g%d_%d" % (i, half), tag)
+            picked[i, half] = g
+            n = HALF // pieces
+            for a in range(0, HALF, n):
+                j0 = half * HALF + a
+                for t in range(PACK):
+                    src = y_sb[t][:].indirect(s_sb[i][:, j0 // 16 : (j0 + n) // 16])
+                    if i == 0:
+                        nc.vector.tensor_copy(g[:, t, a : a + n], src)
+                    else:
+                        nc.vector.tensor_tensor(g[:, t, a : a + n], src, picked[0, half][:, t, a : a + n], SUB)
+
+        def turned(i, jb, extra=None):
+            half, b = divmod(jb, 2)
+            bank = psum_fwd.tile([P, PACK, P], F32, name="b%d_%d" % (i, jb), tag="fwd")
+            for t in range(PACK):
+                sources = [picked[i, half][:, t, b * P : (b + 1) * P]]
+                if extra is not None:
+                    sources.append(extra[t][:, jb * P : (jb + 1) * P])
+                turn(bank[:, t, :], sources)
+            return bank
+
+        rise, base, gain = {}, {}, {}
+
+        def second(jb, tag=None):
+            bank = turned(1, jb)
+            rise[jb] = own([P, PACK, P], F32, "rise_%d" % jb, tag)
+            nc.scalar.activation(rise[jb][:], bank[:], RELU, bias=tr_over[1][:, jb : jb + 1])
+
+        def first(jb):
+            bank = turned(0, jb, c_sb)
+            base[jb] = own([P, PACK, P], F32, "base_%d" % jb)
+            nc.scalar.activation(base[jb][:], bank[:], IDENT, bias=tr_col[0][:, jb : jb + 1])
+
+        def third(jb, bank, tag=None):
+            gain[jb] = own([P, PACK, P], F32, "gain_%d" % jb, tag)
+            nc.vector.scalar_tensor_tensor(
+                gain[jb][:].rearrange("p t m -> p (t m)"),
+                bank[:].rearrange("p t m -> p (t m)"),
+                tr_over[2][:, jb : jb + 1],
+                rise[jb][:].rearrange("p t m -> p (t m)"),
+                ADD, MAX,
             )
 
-        def max12(c):
-            n = CHUNKS[c]
-            state[c, "m"] = work.tile([P, PACK, n], F32, name="m_%d" % c, tag="m")
-            nc.vector.tensor_tensor(state[c, "m"][:], state[c, 0][:], state[c, 1][:], MAX)
-
-        def max3(c):
-            n = CHUNKS[c]
-            state[c, "best"] = work.tile([P, PACK, n], F32, name="best_%d" % c, tag="best")
-            nc.vector.tensor_tensor(state[c, "best"][:], state[c, "m"][:], state[c, 2][:], MAX)
-
-        def weigh(c):
-            n, j0 = CHUNKS[c], starts[c]
-            z = work.tile([P, PACK, n], BF16, name="z_%d" % c, tag="z", align_bytes=64)
-            for t in range(PACK):
-                nc.vector.scalar_tensor_tensor(
-                    z[:, t, :], state[c, "best"][:, t, :], gs_sb[:, t : t + 1],
-                    gc_sb[t][:, j0 : j0 + n], MULT, ADD,
-                )
-            zg = work.tile([P, n, PACK], BF16, name="zg_%d" % c, tag="zg", align_bytes=64)
-            copy = nc.vector.tensor_copy if c == len(CHUNKS) - 1 else nc.scalar.copy
-            copy(
+        def weigh_on_scalar():
+            zg = own([P, HALF, PACK], BF16, "zg_early")
+            z = own([P, PACK, HALF], BF16, "z_early")
+            for t0 in (0, 2):
+                bank = psum.tile([P, 2, HALF], F32, name="back_early_%d" % t0, tag="back")
+                for t in (t0, t0 + 1):
+                    for jb in (0, 1):
+                        turn(bank[:, t - t0, jb * P : (jb + 1) * P], [base[jb][:, t, :], gain[jb][:, t, :]])
+                for t in (t0, t0 + 1):
+                    nc.scalar.activation(z[:, t, :], bank[:, t - t0, :], COPY, scale=gs_sb[:, t : t + 1])
+            nc.scalar.copy(
                 zg[:].rearrange("p (a i) t -> p a t i", i=4),
                 z[:].rearrange("p t (a i) -> p a t i", i=4),
             )
-            state[c, "zg"] = zg
+            return zg
 
-        def score(c):
-            n, j0 = CHUNKS[c], starts[c]
-            z_q = quantize(state[c, "zg"][:].rearrange("p n t -> p (n t)"), n, work, "z%d" % c, "zq")
+        def weigh_on_vector(jb):
+            zg = own([P, P, PACK], BF16, "zg_%d" % jb)
+            bank = psum.tile([P, PACK, P], F32, name="back_%d" % jb, tag="back")
+            for t in range(PACK):
+                turn(bank[:, t, :], [base[jb][:, t, :], gain[jb][:, t, :]])
+            nc.vector.tensor_tensor(
+                zg[:],
+                bank[:].rearrange("p t j -> p j t"),
+                gs_sb[:].unsqueeze(1).to_broadcast([P, P, PACK]),
+                MULT,
+            )
+            return zg
+
+        def score(zg, j0, n):
+            z_q = quantize(zg[:].rearrange("p n t -> p (n t)"), n, keep, "z%d" % j0, "zq%d" % j0)
             per_bank = 512 // n
-            res = work.tile([P, C // P, n], F32, name="res_%d" % c, tag="res")
+            res = own([P, C // P, n], F32, "res_%d" % j0)
             for b0 in range(0, C // P, per_bank):
-                acc = psum.tile([P, per_bank, n], F32, name="o_acc%d_%d" % (c, b0), tag="oacc")
+                acc = psum.tile([P, per_bank, n], F32, name="o_acc%d_%d" % (j0, b0), tag="mx")
                 for b in range(per_bank):
                     product(acc[:, b, :], (cand_words, cand_scales), slice((b0 + b) * P, (b0 + b + 1) * P), z_q)
                 nc.scalar.activation(res[:, b0 : b0 + per_bank, :], acc[:], COPY, scale=0.0625)
             nc.sync.dma_start(out.rearrange("(b p) j -> p b j", p=P)[:, :, j0 : j0 + n], res[:])
 
-        last = len(CHUNKS) - 1
-        for c in range(len(CHUNKS)):
-            for t in range(PACK):
-                gather(c, 0, t)
-                if t == 0 and c > 0:
-                    max3(c - 1)
-                if t == 1 and c > 0:
-                    weigh(c - 1)
-            for t in range(PACK):
-                gather(c, 1, t)
-            if c == 0:
-                emissions()
-            gather(c, 2, 0)
-            max12(c)
-            if c > 0:
-                score(c - 1)
-            for t in range(1, PACK):
-                gather(c, 2, t)
-        max3(last)
-        weigh(last)
-        score(last)
+        gathers(0, 0)
+        gathers(1, 0)
+        emissions()
+        second(0)
+        second(1)
+        gathers(2, 0, tag="w2_grouped")
+        banks = [turned(2, jb) for jb in (0, 1)]
+        gathers(0, 1, tag="w2_raw1")
+        for jb in range(4):
+            first(jb)
+        third(0, banks[0])
+        third(1, banks[1])
+        zg_early = weigh_on_scalar()
+        gathers(1, 1, tag="rise_1")
+        gathers(2, 1, tag="rise_0", pieces=2)
+        second(2, tag="z_early")
+        second(3)
+        banks = [turned(2, jb) for jb in (2, 3)]
+        score(zg_early, 0, HALF)
+        third(2, banks[0], tag="zg_early")
+        third(3, banks[1])
+        for jb in (2, 3):
+            score(weigh_on_vector(jb), jb * P, P)

@@ -32,9 +32,8 @@ def tile_picked_viterb3_none_p_kernel(
     nc = tc.nc
     with ExitStack() as ctx:
         keep = ctx.enter_context(tc.tile_pool(name="keep", bufs=1))
-        work = ctx.enter_context(tc.tile_pool(name="work", bufs=2))
         psum = ctx.enter_context(tc.psum_pool(name="psum", bufs=2))
-        psum_fwd = ctx.enter_context(tc.psum_pool(name="psum_fwd", bufs=4))
+        psum_sum = ctx.enter_context(tc.psum_pool(name="psum_sum", bufs=4))
 
         def load_list(src, name):
             tile = keep.tile([P, S // 16], U16, name=name)
@@ -42,7 +41,7 @@ def tile_picked_viterb3_none_p_kernel(
             return tile
 
         table_scales = keep.tile([P, T], U8, name="table_scales", align_bytes=64)
-        nc.vector.memset(table_scales[:].bitcast(I32), 0)
+        nc.gpsimd.memset(table_scales[:].bitcast(I32), 0)
         offs_sb = load_list(offs, "offs_sb")
         for q in range(4):
             nc.sync.dma_start(
@@ -149,120 +148,126 @@ def tile_picked_viterb3_none_p_kernel(
                 nc.scalar.copy(c_t[:], acc[:])
                 c_sb.append(c_t)
 
-        def turn(dst, sources):
-            for i, src in enumerate(sources):
-                nc.tensor.matmul(dst, src, ident[:], start=(i == 0), stop=(i == len(sources) - 1), is_transpose=True)
-
         def own(shape, dtype, name, tag=None):
             return keep.tile(shape, dtype, name=name, tag=tag or name, align_bytes=64)
 
-        picked = {}
+        def turn(bank, sources, start, stop):
+            for t, src in enumerate(sources):
+                nc.tensor.matmul(
+                    bank[:, t, :], src, ident[:],
+                    start=start and t == 0, stop=stop and t == PACK - 1, is_transpose=True,
+                )
 
-        def gathers(i, half, tag=None, pieces=1):
-            g = own([P, PACK, HALF], F32, "g%d_%d" % (i, half), tag)
-            picked[i, half] = g
-            n = HALF // pieces
-            for a in range(0, HALF, n):
-                j0 = half * HALF + a
-                for t in range(PACK):
-                    src = y_sb[t][:].indirect(s_sb[i][:, j0 // 16 : (j0 + n) // 16])
-                    if i == 0:
-                        nc.vector.tensor_copy(g[:, t, a : a + n], src)
-                    else:
-                        nc.vector.tensor_tensor(g[:, t, a : a + n], src, picked[0, half][:, t, a : a + n], SUB)
-
-        def turned(i, jb, extra=None):
-            half, b = divmod(jb, 2)
-            bank = psum_fwd.tile([P, PACK, P], F32, name="b%d_%d" % (i, jb), tag="fwd")
+        def gather(i, dst, j0, n, first=None):
             for t in range(PACK):
-                sources = [picked[i, half][:, t, b * P : (b + 1) * P]]
-                if extra is not None:
-                    sources.append(extra[t][:, jb * P : (jb + 1) * P])
-                turn(bank[:, t, :], sources)
+                src = y_sb[t][:].indirect(s_sb[i][:, j0 // 16 : (j0 + n) // 16])
+                if first is None:
+                    nc.vector.tensor_copy(dst[:, t, :], src)
+                else:
+                    nc.vector.tensor_tensor(dst[:, t, :], src, first[:, t, :], SUB)
+
+        def block(tile, b):
+            return [tile[:, t, b * P : (b + 1) * P] for t in range(PACK)]
+
+        def quarters(tile):
+            return [tile[:, t, :] for t in range(PACK)]
+
+        NB = S // P
+        y1 = [own([P, PACK, HALF], F32, "y1_%d" % h) for h in range(2)]
+        base_bank = []
+        for h in range(2):
+            gather(0, y1[h], h * HALF, HALF)
+            for b in range(2):
+                bank = psum_sum.tile([P, PACK, P], F32, name="base_bank%d" % (2 * h + b), tag="sum")
+                turn(bank, block(y1[h], b), True, False)
+                base_bank.append(bank)
+
+        emissions()
+        for t in range(PACK):
+            for jb in range(NB):
+                nc.tensor.matmul(
+                    base_bank[jb][:, t, :], c_sb[t][:, jb * P : (jb + 1) * P], ident[:],
+                    start=False, stop=(t == PACK - 1), is_transpose=True,
+                )
+
+        rise, gain, back = {}, {}, {}
+
+        def turned(tile, b, name):
+            bank = psum.tile([P, PACK, P], F32, name=name, tag="diff")
+            turn(bank, block(tile, b), True, True)
             return bank
 
-        rise, base, gain = {}, {}, {}
-
-        def second(jb, tag=None):
-            bank = turned(1, jb)
-            rise[jb] = own([P, PACK, P], F32, "rise_%d" % jb, tag)
+        def second(jb, tile):
+            bank = turned(tile, jb % 2, "d2_bank%d" % jb)
+            rise[jb] = own([P, PACK, P], F32, "rise_%d" % jb)
             nc.scalar.activation(rise[jb][:], bank[:], RELU, bias=tr_over[1][:, jb : jb + 1])
 
         def first(jb):
-            bank = turned(0, jb, c_sb)
-            base[jb] = own([P, PACK, P], F32, "base_%d" % jb)
-            nc.scalar.activation(base[jb][:], bank[:], IDENT, bias=tr_col[0][:, jb : jb + 1])
+            base = own([P, PACK, P], F32, "base_%d" % jb)
+            nc.scalar.activation(base[:], base_bank[jb][:], IDENT, bias=tr_col[0][:, jb : jb + 1])
+            back[jb] = psum_sum.tile([P, PACK, P], F32, name="back%d" % jb, tag="sum")
+            turn(back[jb], quarters(base), True, False)
 
         def third(jb, bank, tag=None):
-            gain[jb] = own([P, PACK, P], F32, "gain_%d" % jb, tag)
+            gain = own([P, PACK, P], F32, "gain_%d" % jb, tag)
             nc.vector.scalar_tensor_tensor(
-                gain[jb][:].rearrange("p t m -> p (t m)"),
+                gain[:].rearrange("p t m -> p (t m)"),
                 bank[:].rearrange("p t m -> p (t m)"),
                 tr_over[2][:, jb : jb + 1],
                 rise[jb][:].rearrange("p t m -> p (t m)"),
                 ADD, MAX,
             )
+            turn(back[jb], quarters(gain), False, True)
 
-        def weigh_on_scalar():
-            zg = own([P, HALF, PACK], BF16, "zg_early")
-            z = own([P, PACK, HALF], BF16, "z_early")
-            for t0 in (0, 2):
-                bank = psum.tile([P, 2, HALF], F32, name="back_early_%d" % t0, tag="back")
-                for t in (t0, t0 + 1):
-                    for jb in (0, 1):
-                        turn(bank[:, t - t0, jb * P : (jb + 1) * P], [base[jb][:, t, :], gain[jb][:, t, :]])
-                for t in (t0, t0 + 1):
-                    nc.scalar.activation(z[:, t, :], bank[:, t - t0, :], COPY, scale=gs_sb[:, t : t + 1])
-            nc.scalar.copy(
-                zg[:].rearrange("p (a i) t -> p a t i", i=4),
-                z[:].rearrange("p t (a i) -> p a t i", i=4),
-            )
-            return zg
-
-        def weigh_on_vector(jb):
-            zg = own([P, P, PACK], BF16, "zg_%d" % jb)
-            bank = psum.tile([P, PACK, P], F32, name="back_%d" % jb, tag="back")
-            for t in range(PACK):
-                turn(bank[:, t, :], [base[jb][:, t, :], gain[jb][:, t, :]])
+        def weigh(jb, zg):
             nc.vector.tensor_tensor(
-                zg[:],
-                bank[:].rearrange("p t j -> p j t"),
+                zg,
+                back[jb][:].rearrange("p t j -> p j t"),
                 gs_sb[:].unsqueeze(1).to_broadcast([P, P, PACK]),
                 MULT,
             )
-            return zg
 
-        def score(zg, j0, n):
+        out_blocks = out.rearrange("(b p) j -> p b j", p=P)
+
+        def score(zg, j0, n, per_bank, tag, last=False):
             z_q = quantize(zg[:].rearrange("p n t -> p (n t)"), n, keep, "z%d" % j0, "zq%d" % j0)
-            per_bank = 512 // n
-            res = own([P, C // P, n], F32, "res_%d" % j0)
             for b0 in range(0, C // P, per_bank):
-                acc = psum.tile([P, per_bank, n], F32, name="o_acc%d_%d" % (j0, b0), tag="mx")
+                acc = psum.tile([P, per_bank, n], F32, name="o_acc%d_%d" % (j0, b0), tag=tag)
                 for b in range(per_bank):
                     product(acc[:, b, :], (cand_words, cand_scales), slice((b0 + b) * P, (b0 + b + 1) * P), z_q)
-                nc.scalar.activation(res[:, b0 : b0 + per_bank, :], acc[:], COPY, scale=0.0625)
-            nc.sync.dma_start(out.rearrange("(b p) j -> p b j", p=P)[:, :, j0 : j0 + n], res[:])
+                res = own([P, per_bank, n], F32, "res_%d_%d" % (j0, b0))
+                if last and b0 > 0:
+                    nc.vector.tensor_scalar(res[:], acc[:], 0.0625, None, MULT)
+                else:
+                    nc.scalar.activation(res[:], acc[:], COPY, scale=0.0625)
+                nc.sync.dma_start(out_blocks[:, b0 : b0 + per_bank, j0 : j0 + n], res[:])
 
-        gathers(0, 0)
-        gathers(1, 0)
-        emissions()
-        second(0)
-        second(1)
-        gathers(2, 0, tag="w2_grouped")
-        banks = [turned(2, jb) for jb in (0, 1)]
-        gathers(0, 1, tag="w2_raw1")
-        for jb in range(4):
+        diffs = own([P, 3, PACK, HALF], F32, "diffs", tag="w2_grouped")
+        gather(1, diffs[:, 0], 0, HALF, y1[0])
+        second(0, diffs[:, 0])
+        second(1, diffs[:, 0])
+        gather(2, diffs[:, 1], 0, HALF, y1[0])
+        banks = [turned(diffs[:, 1], b, "d3_bank%d" % b) for b in range(2)]
+        for jb in range(NB):
             first(jb)
+        gather(1, diffs[:, 2], HALF, HALF, y1[1])
         third(0, banks[0])
         third(1, banks[1])
-        zg_early = weigh_on_scalar()
-        gathers(1, 1, tag="rise_1")
-        gathers(2, 1, tag="rise_0", pieces=2)
-        second(2, tag="z_early")
-        second(3)
-        banks = [turned(2, jb) for jb in (2, 3)]
-        score(zg_early, 0, HALF)
-        third(2, banks[0], tag="zg_early")
-        third(3, banks[1])
+        second(2, diffs[:, 2])
+        second(3, diffs[:, 2])
+        d3_2 = own([P, PACK, P], F32, "d3_2", tag="rise_1")
+        gather(2, d3_2, 2 * P, P, y1[1][:, :, 0:P])
+        zg_early = own([P, HALF, PACK], BF16, "zg_early")
+        weigh(0, zg_early[:, 0:P, :])
+        weigh(1, zg_early[:, P:HALF, :])
+        score(zg_early, 0, HALF, 2, "mx")
+        bank2 = turned(d3_2, 0, "d3_bank2")
+        d3_3 = own([P, PACK, P], F32, "d3_3", tag="zg_early")
+        gather(2, d3_3, 3 * P, P, y1[1][:, :, P:HALF])
+        bank3 = turned(d3_3, 0, "d3_bank3")
+        third(2, bank2, tag="y1_1")
+        third(3, bank3)
         for jb in (2, 3):
-            score(weigh_on_vector(jb), jb * P, P)
+            zg = own([P, P, PACK], BF16, "zg_%d" % jb)
+            weigh(jb, zg[:])
+            score(zg, jb * P, P, 4 if jb == 2 else 2, "mx" if jb == 2 else "diff", last=(jb == 3))

@@ -4,7 +4,7 @@ import concourse.mybir as mybir
 from concourse.masks import make_identity
 
 K, T, S, H, C = 512, 2048, 512, 512, 512
-FLOPS = 3 * 2 * 512 * 512 * 512
+FLOPS = 2 * K * H * S * 2 + 2 * H * C * S
 
 F32 = mybir.dt.float32
 BF16 = mybir.dt.bfloat16
@@ -23,7 +23,12 @@ COPY = mybir.ActivationFunctionType.Copy
 
 P = 128
 PACK = 4
+QUADRANTS = 4
 HALF = S // 2
+W_HALF = H // 2
+EARLY = (0, 1)
+LATE = (2, 3)
+OUT_SCALE = 0.0625
 
 
 def tile_picked_viterb3_none_p_kernel(
@@ -32,78 +37,77 @@ def tile_picked_viterb3_none_p_kernel(
     nc = tc.nc
     with ExitStack() as ctx:
         keep = ctx.enter_context(tc.tile_pool(name="keep", bufs=1))
-        psum = ctx.enter_context(tc.psum_pool(name="psum", bufs=2))
-        psum_sum = ctx.enter_context(tc.psum_pool(name="psum_sum", bufs=4))
+        psum_pairs = ctx.enter_context(tc.psum_pool(name="psum_pairs", bufs=2))
+        psum_single = ctx.enter_context(tc.psum_pool(name="psum_single", bufs=1))
+
+        def own(shape, dtype, name, tag=None):
+            return keep.tile(shape, dtype, name=name, tag=tag or name, align_bytes=64)
 
         def load_list(src, name):
             tile = keep.tile([P, S // 16], U16, name=name)
             nc.sync.dma_start(tile[:], src)
             return tile
 
-        table_scales = keep.tile([P, T], U8, name="table_scales", align_bytes=64)
+        table_scales = own([P, T], U8, "table_scales")
         nc.gpsimd.memset(table_scales[:].bitcast(I32), 0)
         offs_sb = load_list(offs, "offs_sb")
-        for q in range(4):
+        for q in range(QUADRANTS):
             nc.sync.dma_start(
                 table_scales[32 * q : 32 * q + 4, :].bitcast(I32),
                 x_scales[0, 4 * q : 4 * q + 4, :].bitcast(I32),
             )
         two_sb = load_list(two, "two_sb")
         cand_sb = load_list(cand, "cand_sb")
-        table_words = keep.tile([P, T], U32, name="table_words", align_bytes=64)
+        table_words = own([P, T], U32, "table_words")
         nc.sync.dma_start(
             table_words[:].bitcast(I32), x_words[0].rearrange("p n t -> p (n t)").bitcast(I32)
         )
         ident = keep.tile([P, P], F32, name="ident")
         make_identity(nc, ident[:])
 
-        HALVES = 2
-        HC = H // HALVES
-
         def load_weight(w, name):
             rows = w.rearrange("(p j) c -> p j c", j=PACK)
             halves = []
-            for h in range(HALVES):
-                raw = keep.tile([P, PACK, HC], F32, name="%s_raw%d" % (name, h), tag="%s_raw%d" % (name, h), align_bytes=64)
-                nc.sync.dma_start(raw[:], rows[:, :, h * HC : (h + 1) * HC])
+            for h in range(H // W_HALF):
+                raw = own([P, PACK, W_HALF], F32, "%s_raw%d" % (name, h))
+                nc.sync.dma_start(raw[:], rows[:, :, h * W_HALF : (h + 1) * W_HALF])
                 halves.append(raw)
             return halves
 
         w1_raw = load_weight(w1, "w1")
-        s_sb = [load_list(s, "s%d_sb" % i) for i, s in enumerate((s1, s2, s3))]
+        s_sb = [load_list(s, "s%d_sb" % (i + 1)) for i, s in enumerate((s1, s2, s3))]
         w2_raw = load_weight(w2, "w2")
         gs_sb = keep.tile([P, PACK], F32, name="gs_sb")
         nc.sync.dma_start(gs_sb[:], gs.rearrange("(p t) o -> p (t o)", t=PACK))
         tr_col = []
         for i, tr in enumerate((tr1, tr2, tr3)):
-            tile = keep.tile([P, S // P], F32, name="tr%d_col" % i)
+            tile = keep.tile([P, S // P], F32, name="tr%d_col" % (i + 1))
             with nc.allow_non_contiguous_dma(reason="one transition score a partition"):
                 nc.sync.dma_start(tile[:], tr[0].rearrange("(b p) -> p b", p=P))
             tr_col.append(tile)
-        tr_over = [None]
-        for i in (1, 2):
-            tile = keep.tile([P, S // P], F32, name="tr%d_over" % i)
-            nc.gpsimd.tensor_tensor(tile[:], tr_col[i][:], tr_col[0][:], SUB)
-            tr_over.append(tile)
+        tr2_over_tr1 = keep.tile([P, S // P], F32, name="tr2_over_tr1")
+        nc.gpsimd.tensor_tensor(tr2_over_tr1[:], tr_col[1][:], tr_col[0][:], SUB)
+        tr3_over_tr1 = keep.tile([P, S // P], F32, name="tr3_over_tr1")
+        nc.gpsimd.tensor_tensor(tr3_over_tr1[:], tr_col[2][:], tr_col[0][:], SUB)
 
         def pick(table, dtype, idx, name, tag=None):
-            tile = keep.tile([P, S], dtype, name=name, tag=tag or name, align_bytes=64)
+            tile = own([P, S], dtype, name, tag)
             nc.vector.tensor_copy(tile[:], table[:].indirect(idx[:]))
             return tile
 
         def group_weight(halves, name):
-            grouped = keep.tile([P, PACK, P, PACK], BF16, name=name + "_grouped", tag=name + "_grouped", align_bytes=64)
+            grouped = own([P, PACK, P, PACK], BF16, name + "_grouped")
             for h, raw in enumerate(halves):
-                m = slice(h * HC // PACK, (h + 1) * HC // PACK)
+                m = slice(h * W_HALF // PACK, (h + 1) * W_HALF // PACK)
                 nc.scalar.copy(
                     grouped[:, :, m, :].rearrange("p t m j -> p m j t"),
                     raw[:].rearrange("p j (m t) -> p m j t", t=PACK),
                 )
             return grouped
 
-        def quantize(grouped_flat, width, pool, name, tag):
-            codes = pool.tile([P, width], U32, name=name + "_codes", tag=tag + "_codes", align_bytes=64)
-            scales = pool.tile([P, width], U8, name=name + "_scales", tag=tag + "_scales", align_bytes=64)
+        def quantize(grouped_flat, width, name):
+            codes = own([P, width], U32, name + "_codes")
+            scales = own([P, width], U8, name + "_scales")
             nc.vector.quantize_mx(out=codes[:].bitcast(FP8X4), scales=scales[:], in_=grouped_flat)
             return codes, scales
 
@@ -118,6 +122,16 @@ def tile_picked_viterb3_none_p_kernel(
                 stop=True,
             )
 
+        def project(w_q, picked, name):
+            result = []
+            for t in range(PACK):
+                acc = psum_pairs.tile([P, S], F32, name="%s_acc%d" % (name, t), tag="mx")
+                product(acc[:], w_q, slice(t * P, (t + 1) * P), picked)
+                plane = own([P, S], F32, "%s%d" % (name, t))
+                nc.scalar.copy(plane[:], acc[:])
+                result.append(plane)
+            return result
+
         offs_scales = pick(table_scales, U8, offs_sb, "offs_scales")
         two_scales = pick(table_scales, U8, two_sb, "two_scales")
         cand_scales = pick(table_scales, U8, cand_sb, "cand_scales")
@@ -125,149 +139,158 @@ def tile_picked_viterb3_none_p_kernel(
         two_words = pick(table_words, U32, two_sb, "two_words")
 
         w1_grouped = group_weight(w1_raw, "w1")
-        w1_q = quantize(w1_grouped[:].rearrange("p t m j -> p (t m j)"), H, keep, "w1", "w1")
+        w1_q = quantize(w1_grouped[:].rearrange("p t m j -> p (t m j)"), H, "w1")
         cand_words = pick(table_words, U32, cand_sb, "cand_words", tag="w1_grouped")
-
-        y_sb = []
-        for t in range(PACK):
-            acc = psum.tile([P, S], F32, name="y_acc%d" % t, tag="mx")
-            product(acc[:], w1_q, slice(t * P, (t + 1) * P), (offs_words, offs_scales))
-            y = keep.tile([P, S], F32, name="y%d" % t)
-            nc.scalar.copy(y[:], acc[:])
-            y_sb.append(y)
-
+        y_sb = project(w1_q, (offs_words, offs_scales), "y")
         w2_grouped = group_weight(w2_raw, "w2")
-        c_sb = []
 
-        def emissions():
-            w2_q = quantize(w2_grouped[:].rearrange("p t m j -> p (t m j)"), H, keep, "w2", "w2")
-            for t in range(PACK):
-                acc = psum.tile([P, S], F32, name="c_acc%d" % t, tag="mx")
-                product(acc[:], w2_q, slice(t * P, (t + 1) * P), (two_words, two_scales))
-                c_t = keep.tile([P, S], F32, name="c%d" % t)
-                nc.scalar.copy(c_t[:], acc[:])
-                c_sb.append(c_t)
-
-        def own(shape, dtype, name, tag=None):
-            return keep.tile(shape, dtype, name=name, tag=tag or name, align_bytes=64)
-
-        def turn(bank, sources, start, stop):
-            for t, src in enumerate(sources):
-                nc.tensor.matmul(
-                    bank[:, t, :], src, ident[:],
-                    start=start and t == 0, stop=stop and t == PACK - 1, is_transpose=True,
-                )
-
-        def gather(i, dst, j0, n, first=None):
-            for t in range(PACK):
-                src = y_sb[t][:].indirect(s_sb[i][:, j0 // 16 : (j0 + n) // 16])
-                if first is None:
-                    nc.vector.tensor_copy(dst[:, t, :], src)
-                else:
-                    nc.vector.tensor_tensor(dst[:, t, :], src, first[:, t, :], SUB)
-
-        def block(tile, b):
-            return [tile[:, t, b * P : (b + 1) * P] for t in range(PACK)]
-
-        def quarters(tile):
+        def planes(tile):
             return [tile[:, t, :] for t in range(PACK)]
 
-        NB = S // P
-        y1 = [own([P, PACK, HALF], F32, "y1_%d" % h) for h in range(2)]
-        base_bank = []
-        for h in range(2):
-            gather(0, y1[h], h * HALF, HALF)
-            for b in range(2):
-                bank = psum_sum.tile([P, PACK, P], F32, name="base_bank%d" % (2 * h + b), tag="sum")
-                turn(bank, block(y1[h], b), True, False)
-                base_bank.append(bank)
+        def block(views, b):
+            return [view[:, b * P : (b + 1) * P] for view in views]
 
-        emissions()
-        for t in range(PACK):
-            for jb in range(NB):
+        def gather(idx, dst, j0, n, minus=None):
+            for t in range(PACK):
+                src = y_sb[t][:].indirect(idx[:, j0 // 16 : (j0 + n) // 16])
+                if minus is None:
+                    nc.vector.tensor_copy(dst[:, t, :], src)
+                else:
+                    nc.vector.tensor_tensor(dst[:, t, :], src, minus[:, t, :], SUB)
+
+        def turn(places, sources, start, stop):
+            for i, (dst, src) in enumerate(zip(places, sources)):
                 nc.tensor.matmul(
-                    base_bank[jb][:, t, :], c_sb[t][:, jb * P : (jb + 1) * P], ident[:],
-                    start=False, stop=(t == PACK - 1), is_transpose=True,
+                    dst, src, ident[:],
+                    start=start and i == 0, stop=stop and i == len(places) - 1, is_transpose=True,
                 )
 
-        rise, gain, back = {}, {}, {}
-
-        def turned(tile, b, name):
-            bank = psum.tile([P, PACK, P], F32, name=name, tag="diff")
-            turn(bank, block(tile, b), True, True)
+        def turned(views, name, pool, tag):
+            bank = pool.tile([P, PACK, P], F32, name=name, tag=tag)
+            turn(planes(bank), views, True, True)
             return bank
 
-        def second(jb, tile):
-            bank = turned(tile, jb % 2, "d2_bank%d" % jb)
-            rise[jb] = own([P, PACK, P], F32, "rise_%d" % jb)
-            nc.scalar.activation(rise[jb][:], bank[:], RELU, bias=tr_over[1][:, jb : jb + 1])
+        def make_rise(jb, views, bank_tag, tag=None):
+            bank = turned(views, "d2_bank%d" % jb, psum_pairs, bank_tag)
+            rise = own([P, PACK, P], F32, "rise_%d" % jb, tag)
+            nc.scalar.activation(rise[:], bank[:], RELU, bias=tr2_over_tr1[:, jb : jb + 1])
+            return rise
 
-        def first(jb):
+        def make_base(jb, bank, sooner, later):
+            turn(planes(bank), sooner, True, False)
+            turn(planes(bank), later, False, True)
             base = own([P, PACK, P], F32, "base_%d" % jb)
-            nc.scalar.activation(base[:], base_bank[jb][:], IDENT, bias=tr_col[0][:, jb : jb + 1])
-            back[jb] = psum_sum.tile([P, PACK, P], F32, name="back%d" % jb, tag="sum")
-            turn(back[jb], quarters(base), True, False)
+            nc.scalar.activation(base[:], bank[:], IDENT, bias=tr_col[0][:, jb : jb + 1])
+            return base
 
-        def third(jb, bank, tag=None):
-            gain = own([P, PACK, P], F32, "gain_%d" % jb, tag)
+        def make_gain(jb, bank, rise):
+            gain = own([P, PACK, P], F32, "gain_%d" % jb)
             nc.vector.scalar_tensor_tensor(
                 gain[:].rearrange("p t m -> p (t m)"),
                 bank[:].rearrange("p t m -> p (t m)"),
-                tr_over[2][:, jb : jb + 1],
-                rise[jb][:].rearrange("p t m -> p (t m)"),
+                tr3_over_tr1[:, jb : jb + 1],
+                rise[:].rearrange("p t m -> p (t m)"),
                 ADD, MAX,
             )
-            turn(back[jb], quarters(gain), False, True)
+            return gain
 
-        def weigh(jb, zg):
+        out_blocks = out.rearrange("(b p) j -> p b j", p=P)
+
+        def score(z_grouped, j0, n, bank_tag, copies):
+            z_q = quantize(z_grouped[:].rearrange("p n t -> p (n t)"), n, "z%d" % j0)
+            per_bank = C // P // len(copies)
+            for i, copy in enumerate(copies):
+                b0 = i * per_bank
+                acc = psum_pairs.tile([P, per_bank, n], F32, name="o_acc%d_%d" % (j0, b0), tag=bank_tag)
+                for b in range(per_bank):
+                    product(acc[:, b, :], (cand_words, cand_scales), slice((b0 + b) * P, (b0 + b + 1) * P), z_q)
+                res = own([P, per_bank, n], F32, "res_%d_%d" % (j0, b0))
+                copy(res[:], acc[:])
+                nc.sync.dma_start(out_blocks[:, b0 : b0 + per_bank, j0 : j0 + n], res[:])
+
+        def scale_on_scalar(dst, src):
+            nc.scalar.activation(dst, src, COPY, scale=OUT_SCALE)
+
+        def scale_on_vector(dst, src):
+            nc.vector.tensor_scalar(dst, src, OUT_SCALE, None, MULT)
+
+        y1_early = own([P, PACK, HALF], F32, "y1_early")
+        gather(s_sb[0], y1_early, 0, HALF)
+        d2_early = own([P, PACK, HALF], F32, "d2_early")
+        gather(s_sb[1], d2_early, 0, HALF, y1_early)
+        rise = {jb: make_rise(jb, block(planes(d2_early), jb), "diff") for jb in EARLY}
+        w2_q = quantize(w2_grouped[:].rearrange("p t m j -> p (t m j)"), H, "w2")
+        c_sb = project(w2_q, (two_words, two_scales), "c")
+        d3_early = own([P, PACK, HALF], F32, "d3_early", tag="w2_grouped")
+        gather(s_sb[2], d3_early, 0, HALF, y1_early)
+        d3_bank = {
+            jb: turned(block(planes(d3_early), jb), "d3_bank%d" % jb, psum_pairs, "diff") for jb in EARLY
+        }
+        y1_late = own([P, PACK, HALF], F32, "y1_late", tag="w2_raw1")
+        gather(s_sb[0], y1_late, HALF, HALF)
+        base = {}
+        for jb in EARLY:
+            bank = psum_single.tile([P, PACK, P], F32, name="base_bank%d" % jb, tag="sum%d" % jb)
+            base[jb] = make_base(jb, bank, block(planes(y1_early), jb), block(c_sb, jb))
+        for b, jb in enumerate(LATE):
+            bank = psum_pairs.tile([P, PACK, P], F32, name="base_bank%d" % jb, tag="mx")
+            base[jb] = make_base(jb, bank, block(c_sb, jb), block(planes(y1_late), b))
+
+        early = [psum_single.tile([P, 2, 2, P], F32, name="early%d" % u, tag="early%d" % u) for u in range(2)]
+
+        def turn_early(jb, tile, start, stop):
+            for u in range(2):
+                turn(
+                    [early[u][:, e, jb, :] for e in range(2)],
+                    [tile[:, 2 * u + e, :] for e in range(2)],
+                    start, stop,
+                )
+
+        for jb in EARLY:
+            turn_early(jb, base[jb], jb == EARLY[0], False)
+        for jb in EARLY:
+            turn_early(jb, make_gain(jb, d3_bank[jb], rise[jb]), False, jb == EARLY[-1])
+        z_early = own([P, PACK, HALF], BF16, "z_early")
+        for t in range(PACK):
+            nc.scalar.activation(
+                z_early[:, t, :],
+                early[t // 2][:, t % 2].rearrange("p b j -> p (b j)"),
+                COPY,
+                scale=gs_sb[:, t : t + 1],
+            )
+        zg_early = own([P, HALF, PACK], BF16, "zg_early")
+        nc.scalar.copy(
+            zg_early[:].rearrange("p (a i) t -> p a t i", i=4),
+            z_early[:].rearrange("p t (a i) -> p a t i", i=4),
+        )
+
+        late = own([P, 2, PACK * HALF], F32, "late", tag="rise_1")
+        d2_late = late[:, 0].rearrange("p (t j) -> p t j", t=PACK)
+        gather(s_sb[1], d2_late, HALF, HALF, y1_late)
+        for b, jb in enumerate(LATE):
+            rise[jb] = make_rise(jb, block(planes(d2_late), b), "mx", tag="gain_%d" % (1 - b))
+        back = {}
+        for b, jb in enumerate(LATE):
+            back[jb] = psum_single.tile([P, PACK, P], F32, name="back%d" % jb, tag="sum%d" % b)
+            turn(planes(back[jb]), planes(base[jb]), True, False)
+        d3_late = late[:, 1].rearrange("p (b t j) -> p b t j", b=2, t=PACK)
+        for b, jb in enumerate(LATE):
+            gather(s_sb[2], d3_late[:, b], jb * P, P, y1_late[:, :, b * P : (b + 1) * P])
+        for b, jb in enumerate(LATE):
+            d3_bank[jb] = turned(planes(d3_late[:, b]), "d3_bank%d" % jb, psum_single, "early%d" % b)
+        for jb in LATE:
+            turn(planes(back[jb]), planes(make_gain(jb, d3_bank[jb], rise[jb])), False, True)
+
+        def weigh_on_vector(jb, tag=None):
+            zg = own([P, P, PACK], BF16, "zg_%d" % jb, tag)
             nc.vector.tensor_tensor(
-                zg,
+                zg[:],
                 back[jb][:].rearrange("p t j -> p j t"),
                 gs_sb[:].unsqueeze(1).to_broadcast([P, P, PACK]),
                 MULT,
             )
+            return zg
 
-        out_blocks = out.rearrange("(b p) j -> p b j", p=P)
-
-        def score(zg, j0, n, per_bank, tag, last=False):
-            z_q = quantize(zg[:].rearrange("p n t -> p (n t)"), n, keep, "z%d" % j0, "zq%d" % j0)
-            for b0 in range(0, C // P, per_bank):
-                acc = psum.tile([P, per_bank, n], F32, name="o_acc%d_%d" % (j0, b0), tag=tag)
-                for b in range(per_bank):
-                    product(acc[:, b, :], (cand_words, cand_scales), slice((b0 + b) * P, (b0 + b + 1) * P), z_q)
-                res = own([P, per_bank, n], F32, "res_%d_%d" % (j0, b0))
-                if last and b0 > 0:
-                    nc.vector.tensor_scalar(res[:], acc[:], 0.0625, None, MULT)
-                else:
-                    nc.scalar.activation(res[:], acc[:], COPY, scale=0.0625)
-                nc.sync.dma_start(out_blocks[:, b0 : b0 + per_bank, j0 : j0 + n], res[:])
-
-        diffs = own([P, 3, PACK, HALF], F32, "diffs", tag="w2_grouped")
-        gather(1, diffs[:, 0], 0, HALF, y1[0])
-        second(0, diffs[:, 0])
-        second(1, diffs[:, 0])
-        gather(2, diffs[:, 1], 0, HALF, y1[0])
-        banks = [turned(diffs[:, 1], b, "d3_bank%d" % b) for b in range(2)]
-        for jb in range(NB):
-            first(jb)
-        gather(1, diffs[:, 2], HALF, HALF, y1[1])
-        third(0, banks[0])
-        third(1, banks[1])
-        second(2, diffs[:, 2])
-        second(3, diffs[:, 2])
-        d3_2 = own([P, PACK, P], F32, "d3_2", tag="rise_1")
-        gather(2, d3_2, 2 * P, P, y1[1][:, :, 0:P])
-        zg_early = own([P, HALF, PACK], BF16, "zg_early")
-        weigh(0, zg_early[:, 0:P, :])
-        weigh(1, zg_early[:, P:HALF, :])
-        score(zg_early, 0, HALF, 2, "mx")
-        bank2 = turned(d3_2, 0, "d3_bank2")
-        d3_3 = own([P, PACK, P], F32, "d3_3", tag="zg_early")
-        gather(2, d3_3, 3 * P, P, y1[1][:, :, P:HALF])
-        bank3 = turned(d3_3, 0, "d3_bank3")
-        third(2, bank2, tag="y1_1")
-        third(3, bank3)
-        for jb in (2, 3):
-            zg = own([P, P, PACK], BF16, "zg_%d" % jb)
-            weigh(jb, zg[:])
-            score(zg, jb * P, P, 4 if jb == 2 else 2, "mx" if jb == 2 else "diff", last=(jb == 3))
+        score(zg_early, 0, HALF, "mx", (scale_on_scalar, scale_on_scalar))
+        score(weigh_on_vector(LATE[0], tag="zg_early"), LATE[0] * P, P, "mx", (scale_on_scalar,))
+        score(weigh_on_vector(LATE[1]), LATE[1] * P, P, "diff", (scale_on_scalar, scale_on_vector))

from contextlib import ExitStack

import concourse.mybir as mybir
from concourse.masks import make_identity

K, T, S, H, C = 512, 2048, 512, 512, 512
FLOPS = 2 * K * H * S * 2 + 2 * H * C * S

F32 = mybir.dt.float32
BF16 = mybir.dt.bfloat16
I32 = mybir.dt.int32
U32 = mybir.dt.uint32
U16 = mybir.dt.uint16
U8 = mybir.dt.uint8
FP8X4 = mybir.dt.float8_e4m3fn_x4
ADD = mybir.AluOpType.add
MULT = mybir.AluOpType.mult
MAX = mybir.AluOpType.max
SUB = mybir.AluOpType.subtract
RELU = mybir.ActivationFunctionType.Relu
IDENT = mybir.ActivationFunctionType.Identity
COPY = mybir.ActivationFunctionType.Copy

P = 128
PACK = 4
QUADRANTS = 4
HALF = S // 2
W_HALF = H // 2
EARLY = (0, 1)
LATE = (2, 3)
OUT_SCALE = 0.0625


def tile_picked_viterb3_none_p_kernel(
    tc, x_words, x_scales, w1, w2, tr1, tr2, tr3, gs, offs, two, s1, s2, s3, cand, out
):
    nc = tc.nc
    with ExitStack() as ctx:
        keep = ctx.enter_context(tc.tile_pool(name="keep", bufs=1))
        psum_pairs = ctx.enter_context(tc.psum_pool(name="psum_pairs", bufs=2))
        psum_single = ctx.enter_context(tc.psum_pool(name="psum_single", bufs=1))

        def own(shape, dtype, name, tag=None):
            return keep.tile(shape, dtype, name=name, tag=tag or name, align_bytes=64)

        def load_list(src, name):
            tile = keep.tile([P, S // 16], U16, name=name)
            nc.sync.dma_start(tile[:], src)
            return tile

        table_scales = own([P, T], U8, "table_scales")
        nc.gpsimd.memset(table_scales[:].bitcast(I32), 0)
        offs_sb = load_list(offs, "offs_sb")
        for q in range(QUADRANTS):
            nc.sync.dma_start(
                table_scales[32 * q : 32 * q + 4, :].bitcast(I32),
                x_scales[0, 4 * q : 4 * q + 4, :].bitcast(I32),
            )
        two_sb = load_list(two, "two_sb")
        cand_sb = load_list(cand, "cand_sb")
        table_words = own([P, T], U32, "table_words")
        nc.sync.dma_start(
            table_words[:].bitcast(I32), x_words[0].rearrange("p n t -> p (n t)").bitcast(I32)
        )
        ident = keep.tile([P, P], F32, name="ident")
        make_identity(nc, ident[:])

        def load_weight(w, name):
            rows = w.rearrange("(p j) c -> p j c", j=PACK)
            halves = []
            for h in range(H // W_HALF):
                raw = own([P, PACK, W_HALF], F32, "%s_raw%d" % (name, h))
                nc.sync.dma_start(raw[:], rows[:, :, h * W_HALF : (h + 1) * W_HALF])
                halves.append(raw)
            return halves

        w1_raw = load_weight(w1, "w1")
        s_sb = [load_list(s, "s%d_sb" % (i + 1)) for i, s in enumerate((s1, s2, s3))]
        w2_raw = load_weight(w2, "w2")
        gs_sb = keep.tile([P, PACK], F32, name="gs_sb")
        nc.sync.dma_start(gs_sb[:], gs.rearrange("(p t) o -> p (t o)", t=PACK))
        tr_col = []
        for i, tr in enumerate((tr1, tr2, tr3)):
            tile = keep.tile([P, S // P], F32, name="tr%d_col" % (i + 1))
            with nc.allow_non_contiguous_dma(reason="one transition score a partition"):
                nc.sync.dma_start(tile[:], tr[0].rearrange("(b p) -> p b", p=P))
            tr_col.append(tile)
        tr2_over_tr1 = keep.tile([P, S // P], F32, name="tr2_over_tr1")
        nc.gpsimd.tensor_tensor(tr2_over_tr1[:], tr_col[1][:], tr_col[0][:], SUB)
        tr3_over_tr1 = keep.tile([P, S // P], F32, name="tr3_over_tr1")
        nc.gpsimd.tensor_tensor(tr3_over_tr1[:], tr_col[2][:], tr_col[0][:], SUB)

        def pick(table, dtype, idx, name, tag=None):
            tile = own([P, S], dtype, name, tag)
            nc.vector.tensor_copy(tile[:], table[:].indirect(idx[:]))
            return tile

        def group_weight(halves, name):
            grouped = own([P, PACK, P, PACK], BF16, name + "_grouped")
            for h, raw in enumerate(halves):
                m = slice(h * W_HALF // PACK, (h + 1) * W_HALF // PACK)
                nc.scalar.copy(
                    grouped[:, :, m, :].rearrange("p t m j -> p m j t"),
                    raw[:].rearrange("p j (m t) -> p m j t", t=PACK),
                )
            return grouped

        def quantize(grouped_flat, width, name):
            codes = own([P, width], U32, name + "_codes")
            scales = own([P, width], U8, name + "_scales")
            nc.vector.quantize_mx(out=codes[:].bitcast(FP8X4), scales=scales[:], in_=grouped_flat)
            return codes, scales

        def product(acc, lhs, lhs_cols, rhs):
            nc.tensor.matmul_mx(
                out=acc,
                lhsT=lhs[0][:, lhs_cols].bitcast(FP8X4),
                lhsT_scale=lhs[1][:, lhs_cols],
                rhs=rhs[0][:].bitcast(FP8X4),
                rhs_scale=rhs[1][:],
                start=True,
                stop=True,
            )

        def project(w_q, picked, name):
            result = []
            for t in range(PACK):
                acc = psum_pairs.tile([P, S], F32, name="%s_acc%d" % (name, t), tag="mx")
                product(acc[:], w_q, slice(t * P, (t + 1) * P), picked)
                plane = own([P, S], F32, "%s%d" % (name, t))
                nc.scalar.copy(plane[:], acc[:])
                result.append(plane)
            return result

        offs_scales = pick(table_scales, U8, offs_sb, "offs_scales")
        two_scales = pick(table_scales, U8, two_sb, "two_scales")
        cand_scales = pick(table_scales, U8, cand_sb, "cand_scales")
        offs_words = pick(table_words, U32, offs_sb, "offs_words")
        two_words = pick(table_words, U32, two_sb, "two_words")

        w1_grouped = group_weight(w1_raw, "w1")
        w1_q = quantize(w1_grouped[:].rearrange("p t m j -> p (t m j)"), H, "w1")
        cand_words = pick(table_words, U32, cand_sb, "cand_words", tag="w1_grouped")
        y_sb = project(w1_q, (offs_words, offs_scales), "y")
        w2_grouped = group_weight(w2_raw, "w2")

        def planes(tile):
            return [tile[:, t, :] for t in range(PACK)]

        def block(views, b):
            return [view[:, b * P : (b + 1) * P] for view in views]

        def gather(idx, dst, j0, n, minus=None):
            for t in range(PACK):
                src = y_sb[t][:].indirect(idx[:, j0 // 16 : (j0 + n) // 16])
                if minus is None:
                    nc.vector.tensor_copy(dst[:, t, :], src)
                else:
                    nc.vector.tensor_tensor(dst[:, t, :], src, minus[:, t, :], SUB)

        def turn(places, sources, start, stop):
            for i, (dst, src) in enumerate(zip(places, sources)):
                nc.tensor.matmul(
                    dst, src, ident[:],
                    start=start and i == 0, stop=stop and i == len(places) - 1, is_transpose=True,
                )

        def turned(views, name, pool, tag):
            bank = pool.tile([P, PACK, P], F32, name=name, tag=tag)
            turn(planes(bank), views, True, True)
            return bank

        def make_rise(jb, views, bank_tag, tag=None):
            bank = turned(views, "d2_bank%d" % jb, psum_pairs, bank_tag)
            rise = own([P, PACK, P], F32, "rise_%d" % jb, tag)
            nc.scalar.activation(rise[:], bank[:], RELU, bias=tr2_over_tr1[:, jb : jb + 1])
            return rise

        def make_base(jb, bank, sooner, later):
            turn(planes(bank), sooner, True, False)
            turn(planes(bank), later, False, True)
            base = own([P, PACK, P], F32, "base_%d" % jb)
            nc.scalar.activation(base[:], bank[:], IDENT, bias=tr_col[0][:, jb : jb + 1])
            return base

        def make_gain(jb, bank, rise):
            gain = own([P, PACK, P], F32, "gain_%d" % jb)
            nc.vector.scalar_tensor_tensor(
                gain[:].rearrange("p t m -> p (t m)"),
                bank[:].rearrange("p t m -> p (t m)"),
                tr3_over_tr1[:, jb : jb + 1],
                rise[:].rearrange("p t m -> p (t m)"),
                ADD, MAX,
            )
            return gain

        out_blocks = out.rearrange("(b p) j -> p b j", p=P)

        def score(z_grouped, j0, n, bank_tag, copies):
            z_q = quantize(z_grouped[:].rearrange("p n t -> p (n t)"), n, "z%d" % j0)
            per_bank = C // P // len(copies)
            for i, copy in enumerate(copies):
                b0 = i * per_bank
                acc = psum_pairs.tile([P, per_bank, n], F32, name="o_acc%d_%d" % (j0, b0), tag=bank_tag)
                for b in range(per_bank):
                    product(acc[:, b, :], (cand_words, cand_scales), slice((b0 + b) * P, (b0 + b + 1) * P), z_q)
                res = own([P, per_bank, n], F32, "res_%d_%d" % (j0, b0))
                copy(res[:], acc[:])
                nc.sync.dma_start(out_blocks[:, b0 : b0 + per_bank, j0 : j0 + n], res[:])

        def scale_on_scalar(dst, src):
            nc.scalar.activation(dst, src, COPY, scale=OUT_SCALE)

        def scale_on_vector(dst, src):
            nc.vector.tensor_scalar(dst, src, OUT_SCALE, None, MULT)

        y1_early = own([P, PACK, HALF], F32, "y1_early")
        gather(s_sb[0], y1_early, 0, HALF)
        d2_early = own([P, PACK, HALF], F32, "d2_early")
        gather(s_sb[1], d2_early, 0, HALF, y1_early)
        rise = {jb: make_rise(jb, block(planes(d2_early), jb), "diff") for jb in EARLY}
        w2_q = quantize(w2_grouped[:].rearrange("p t m j -> p (t m j)"), H, "w2")
        c_sb = project(w2_q, (two_words, two_scales), "c")
        d3_early = own([P, PACK, HALF], F32, "d3_early", tag="w2_grouped")
        gather(s_sb[2], d3_early, 0, HALF, y1_early)
        d3_bank = {
            jb: turned(block(planes(d3_early), jb), "d3_bank%d" % jb, psum_pairs, "diff") for jb in EARLY
        }
        y1_late = own([P, PACK, HALF], F32, "y1_late", tag="w2_raw1")
        gather(s_sb[0], y1_late, HALF, HALF)
        base = {}
        for jb in EARLY:
            bank = psum_single.tile([P, PACK, P], F32, name="base_bank%d" % jb, tag="sum%d" % jb)
            base[jb] = make_base(jb, bank, block(planes(y1_early), jb), block(c_sb, jb))
        for b, jb in enumerate(LATE):
            bank = psum_pairs.tile([P, PACK, P], F32, name="base_bank%d" % jb, tag="mx")
            base[jb] = make_base(jb, bank, block(c_sb, jb), block(planes(y1_late), b))

        early = [psum_single.tile([P, 2, 2, P], F32, name="early%d" % u, tag="early%d" % u) for u in range(2)]

        def turn_early(jb, tile, start, stop):
            for u in range(2):
                turn(
                    [early[u][:, e, jb, :] for e in range(2)],
                    [tile[:, 2 * u + e, :] for e in range(2)],
                    start, stop,
                )

        for jb in EARLY:
            turn_early(jb, base[jb], jb == EARLY[0], False)
        for jb in EARLY:
            turn_early(jb, make_gain(jb, d3_bank[jb], rise[jb]), False, jb == EARLY[-1])
        z_early = own([P, PACK, HALF], BF16, "z_early")
        for t in range(PACK):
            nc.scalar.activation(
                z_early[:, t, :],
                early[t // 2][:, t % 2].rearrange("p b j -> p (b j)"),
                COPY,
                scale=gs_sb[:, t : t + 1],
            )
        zg_early = own([P, HALF, PACK], BF16, "zg_early")
        nc.scalar.copy(
            zg_early[:].rearrange("p (a i) t -> p a t i", i=4),
            z_early[:].rearrange("p t (a i) -> p a t i", i=4),
        )

        late = own([P, 2, PACK * HALF], F32, "late", tag="rise_1")
        d2_late = late[:, 0].rearrange("p (t j) -> p t j", t=PACK)
        gather(s_sb[1], d2_late, HALF, HALF, y1_late)
        for b, jb in enumerate(LATE):
            rise[jb] = make_rise(jb, block(planes(d2_late), b), "mx", tag="gain_%d" % (1 - b))
        back = {}
        for b, jb in enumerate(LATE):
            back[jb] = psum_single.tile([P, PACK, P], F32, name="back%d" % jb, tag="sum%d" % b)
            turn(planes(back[jb]), planes(base[jb]), True, False)
        d3_late = late[:, 1].rearrange("p (b t j) -> p b t j", b=2, t=PACK)
        for b, jb in enumerate(LATE):
            gather(s_sb[2], d3_late[:, b], jb * P, P, y1_late[:, :, b * P : (b + 1) * P])
        for b, jb in enumerate(LATE):
            d3_bank[jb] = turned(planes(d3_late[:, b]), "d3_bank%d" % jb, psum_single, "early%d" % b)
        for jb in LATE:
            turn(planes(back[jb]), planes(make_gain(jb, d3_bank[jb], rise[jb])), False, True)

        def weigh_on_vector(jb, tag=None):
            zg = own([P, P, PACK], BF16, "zg_%d" % jb, tag)
            nc.vector.tensor_tensor(
                zg[:],
                back[jb][:].rearrange("p t j -> p j t"),
                gs_sb[:].unsqueeze(1).to_broadcast([P, P, PACK]),
                MULT,
            )
            return zg

        score(zg_early, 0, HALF, "mx", (scale_on_scalar, scale_on_scalar))
        score(weigh_on_vector(LATE[0], tag="zg_early"), LATE[0] * P, P, "mx", (scale_on_scalar,))
        score(weigh_on_vector(LATE[1]), LATE[1] * P, P, "diff", (scale_on_scalar, scale_on_vector))
